import numpy as np
import ml_dtypes


def mxq(x, axis, fmt="e4m3"):
    dtype, down = {"e4m3": (ml_dtypes.float8_e4m3fn, 7), "e5m2": (ml_dtypes.float8_e5m2, 14)}[fmt]
    v = np.moveaxis(np.asarray(x, np.float32).astype(ml_dtypes.bfloat16).astype(np.float64), axis, -1)
    blocks = v.reshape(v.shape[:-1] + (-1, 32))
    amax = np.abs(blocks).max(-1, keepdims=True)
    byte = np.maximum(np.where(amax > 0, np.frexp(amax)[1] - 1 + 127, 0) - down, 1)
    scale = np.exp2(byte - 127.0)
    codes = (blocks / scale).astype(np.float32).astype(dtype).astype(np.float64)
    return np.moveaxis((codes * scale).reshape(v.shape), -1, axis)


WIDE = False


def mx_kscale(k):
    if not WIDE:
        return np.ones(k)
    levels = np.array([10, -10, 5, -5, 0])
    if k % 512:
        return np.exp2(np.random.permutation(np.resize(levels, k // 32))).repeat(32)
    a = np.empty((k // 512, 16))
    for p in range(k // 512):
        a[p, :8] = np.random.permutation(np.resize(levels, 8))
        for g in range(8):
            far = levels[np.abs(levels - a[p, g]) >= 10]
            a[p, g + 8] = far[np.random.randint(len(far))]
    return np.exp2(a.ravel()).repeat(32)


def f64(x):
    return np.asarray(x).astype(np.float64)


def striped(idx):
    return np.tile(idx.reshape(-1, 16).T, (8, 1)).astype(np.uint16)


def unstriped(offs):
    return offs[:16].T.reshape(-1).astype(np.int64)


def striped8(idx):
    return np.concatenate([x.reshape(-1, 16).T for x in idx]).astype(np.uint16)


def runs(offs, k):
    lists = np.stack([offs[16 * r : 16 * r + 16].T.reshape(-1) for r in range(8)]).astype(np.int64)
    return lists[np.arange(k) % 512 // 64]


def pack_weight(w):
    k, n = w.shape
    w = f64(np.asarray(w, np.float32).astype(ml_dtypes.bfloat16)).reshape(k // 32, 32, n)
    amax = np.abs(w).max(1)
    byte = np.clip(np.where(amax > 0, np.frexp(amax)[1] - 1 + 127 - 7, 1), 1, 254)
    scaled = (w * np.exp2(127.0 - byte)[:, None, :]).reshape(k, n).astype(np.float32)
    words = np.ascontiguousarray(scaled.reshape(k // 512, 128, 4, n).transpose(0, 1, 3, 2)).astype(ml_dtypes.float8_e4m3fn).view(np.uint8)
    return words, np.ascontiguousarray(byte.astype(np.uint8).reshape(k // 512, 16, n))


def unpack_weight(words, scales):
    g, p, n, _ = words.shape
    vals = np.ascontiguousarray(words).view(ml_dtypes.float8_e4m3fn).astype(np.float64) * np.repeat(np.exp2(scales.astype(np.float64) - 127.0), 8, axis=1)[..., None]
    return vals.transpose(0, 1, 3, 2).reshape(g * 512, n)

def planes(y):
    n, m = y.shape
    v = y.astype(np.float32).astype(ml_dtypes.bfloat16).astype(np.float64).reshape(n // 32, 32, m)
    top = np.abs(v).max(1)
    byte = np.clip(np.where(top > 0, np.frexp(top)[1] - 1 + 127 - 7, 1), 1, 254)
    codes = (v * np.exp2(127.0 - byte)[:, None, :]).reshape(n, m).astype(np.float32).astype(ml_dtypes.float8_e4m3fn).view(np.uint8)
    words = codes.reshape(n // 512, 128, 4, m).transpose(0, 1, 3, 2)
    return np.ascontiguousarray(words), np.ascontiguousarray(byte.astype(np.uint8).reshape(n // 512, 16, m))


K, T, S, H, C = 512, 2048, 256, 512, 512


def setup_inputs():
    n = np.random.standard_normal
    s = mx_kscale(K)[:, None]
    packed_xT = pack_weight(n((K, T)) * s)
    packed_w1 = pack_weight(n((K, H)) / np.sqrt(K) / s)
    return {
        "x_words": packed_xT[0],
        "x_scales": packed_xT[1],
        "w1_words": packed_w1[0],
        "w1_scales": packed_w1[1],
        "gs": (np.random.uniform(0.5, 1.5, (K, 1)) / s).astype(np.float32),
        "offs": striped(np.random.permutation(T)[:S]),
        "n1": striped8(np.stack([np.random.permutation(S) for _ in range(8)])),
        "n2": striped8(np.stack([np.random.permutation(S) for _ in range(8)])),
        "ca": striped(np.random.permutation(T)[:C]),
        "hc": striped8(np.random.randint(0, T, (8, C))),
        "n3": striped8(np.stack([np.random.permutation(S) for _ in range(8)])),
        "n4": striped8(np.stack([np.random.permutation(S) for _ in range(8)])),
        "n5": striped8(np.stack([np.random.permutation(S) for _ in range(8)])),
        "n6": striped8(np.stack([np.random.permutation(S) for _ in range(8)])),
    }


def reference(x_words, x_scales, w1_words, w1_scales, gs, offs, n1, n2, ca, hc, n3, n4, n5, n6):
    x_ca = unpack_weight(x_words, x_scales)[:, unstriped(ca)]
    xq = unpack_weight(x_words, x_scales)[:, unstriped(offs)]
    y = unpack_weight(w1_words, w1_scales).T @ xq
    z = f64(gs) * (y[np.arange(H)[:, None], runs(n1, H)] + 0.75 * (y[np.arange(H)[:, None], runs(n2, H)]))
    zq = mxq(z, 0, "e4m3")
    a = 0.0625 * (x_ca.T @ zq)
    x_hc = unpack_weight(x_words, x_scales)[np.arange(K)[:, None], runs(hc, K)]
    b = 0.0625 * (x_hc.T @ zq)
    out_0 = np.maximum(a[np.arange(C)[:, None], runs(n3, C)] + b[np.arange(C)[:, None], runs(n5, C)], a[np.arange(C)[:, None], runs(n4, C)] + b[np.arange(C)[:, None], runs(n6, C)])
    return (out_0,) + planes(out_0)

@@ -1,0 +1,232 @@
+from contextlib import ExitStack
+
+import concourse.mybir as mybir
+
+K, T, S, H, C = 512, 2048, 256, 512, 512
+FLOPS = 2 * K * S * (H + 2 * C)
+
+F32 = mybir.dt.float32
+BF16 = mybir.dt.bfloat16
+I32 = mybir.dt.int32
+U32 = mybir.dt.uint32
+U16 = mybir.dt.uint16
+U8 = mybir.dt.uint8
+FP8X4 = mybir.dt.float8_e4m3fn_x4
+COPY = mybir.ActivationFunctionType.Copy
+ALU = mybir.AluOpType
+
+P = 128
+PACK = 4
+PER_COL = 16
+CODE_GATHER = 256
+Z_PIECES = [128,128]
+OUT_PIECES = [128,64,64]
+
+
+def pieces(widths):
+    starts = [sum(widths[:i]) for i in range(len(widths))]
+    return [slice(a, a + w) for a, w in zip(starts, widths)]
+
+
+def offsets(lst, cols):
+    return lst[:, cols.start // PER_COL : cols.stop // PER_COL]
+
+
+def tile_picked_cdhpathbsum_none_po_kernel(
+    tc, x_words, x_scales, w1_words, w1_scales, gs, offs, n1, n2, ca, hc, n3, n4, n5, n6, out_0, out_1, out_2
+):
+    nc = tc.nc
+    with ExitStack() as ctx:
+        keep = ctx.enter_context(tc.tile_pool(name="keep", bufs=1))
+        psum = ctx.enter_context(tc.psum_pool(name="psum", bufs=1))
+
+        def sb(name, shape, dtype, tag=""):
+            return keep.tile(shape, dtype, name=name, tag=tag or name, align_bytes=64)
+
+        def bank(name, tag, shape):
+            return psum.tile(shape, F32, name=name, tag=tag)
+
+        def load_list(name, src):
+            lst = sb(name, [P, src.shape[1]], U16)
+            nc.sync.dma_start(lst[:], src)
+            return lst
+
+        xs = sb("xs", [P, T], U8)
+        ws = sb("ws", [P, H], U8)
+        xw = sb("xw", [P, T], U32)
+        ww = sb("ww", [P, H], U32)
+        gain = sb("gain", [P, PACK], F32)
+        nc.vector.memset(xs[:].bitcast(I32), 0)
+        nc.vector.memset(ws[:].bitcast(I32), 0)
+        xs_rows = x_scales[0].bitcast(I32)
+        ws_rows = w1_scales[0].bitcast(I32)
+        l_offs = load_list("l_offs", offs)
+        l_hc = load_list("l_hc", hc)
+        nc.sync.dma_start(ww[:].bitcast(I32), w1_words[0].rearrange("p c r -> p (c r)").bitcast(I32))
+        nc.scalar.dma_start(xs[0:P:16, :].bitcast(I32), xs_rows[0:16:2, :])
+        nc.sync.dma_start(xs[1:P:16, :].bitcast(I32), xs_rows[1:16:2, :])
+        nc.scalar.dma_start(xs[2:P:32, :].bitcast(I32), xs_rows[2:16:4, :])
+        nc.sync.dma_start(xs[3:P:32, :].bitcast(I32), xs_rows[3:16:4, :])
+        nc.sync.dma_start(xw[:].bitcast(I32), x_words[0].rearrange("p c r -> p (c r)").bitcast(I32))
+        for q in range(4):
+            nc.sync.dma_start(ws[32 * q : 32 * q + 4, :].bitcast(I32), ws_rows[4 * q : 4 * q + 4, :])
+        nc.sync.dma_start(gain[:], gs.rearrange("(p t) o -> p (t o)", t=PACK))
+        l1 = load_list("l1", n1)
+        l_ca = load_list("l_ca", ca)
+        l2 = load_list("l2", n2)
+        l3 = load_list("l3", n3)
+        l4 = load_list("l4", n4)
+        l5 = load_list("l5", n5)
+        l6 = load_list("l6", n6)
+
+        def gather_codes(name, table, lst, n, dtype, tag=""):
+            got = sb(name, [P, n], dtype, tag)
+            for cols in pieces([CODE_GATHER] * (n // CODE_GATHER)):
+                nc.vector.tensor_copy(got[:, cols], table[:].indirect(offsets(lst, cols)))
+            return got
+
+        def deal_words(name, src):
+            dealt = sb(name, [P, C], U32)
+            nc.vector.tensor_copy(
+                dealt[:].bitcast(I32).rearrange("p (t m) -> p m t", t=PACK),
+                src[:].bitcast(I32).rearrange("p (m t) -> p m t", t=PACK),
+            )
+            return dealt
+
+        def deal_bytes(name, src, groups=(slice(0, PACK),)):
+            dealt = sb(name, [P, C], U8)
+            for ts in groups:
+                nc.vector.tensor_copy(
+                    dealt[:].rearrange("p (t m) -> p t m", t=PACK)[:, ts, :],
+                    src[:].rearrange("p (m t) -> p t m", t=PACK)[:, ts, :],
+                )
+            return dealt
+
+        def product(out, words, scales, t, mov_words, mov_scales):
+            rows = slice(t * P, (t + 1) * P)
+            nc.tensor.matmul_mx(
+                out=out,
+                lhsT=words[:, rows].bitcast(FP8X4),
+                lhsT_scale=scales[:, rows],
+                rhs=mov_words.bitcast(FP8X4),
+                rhs_scale=mov_scales,
+                start=True,
+                stop=True,
+            )
+
+        def round_and_quantize(name, planes, cols, words, scales):
+            rounded = sb(name, [P, cols.stop - cols.start, PACK], BF16)
+            nc.vector.tensor_copy(
+                rounded[:].rearrange("p (c i) t -> p c t i", i=4),
+                planes[:, :, cols].rearrange("p t (c i) -> p c t i", i=4),
+            )
+            nc.vector.quantize_mx(
+                out=words[:, cols].bitcast(FP8X4),
+                scales=scales[:, cols],
+                in_=rounded[:].rearrange("p n t -> p (n t)"),
+            )
+
+        def fetch(dst, window, lst, cols):
+            table = window[:] if cols.stop - cols.start >= P else window[:, :S]
+            nc.scalar.activation(dst, table.indirect(offsets(lst, cols)), COPY)
+
+        everything = slice(0, S)
+        last_t = PACK - 1
+
+        ys = [sb("y%d" % t, [P, 2 * S], F32) for t in range(PACK)]
+        for y in ys:
+            nc.vector.memset(y[:, S:], 0.0)
+        xq_w = gather_codes("xq_w", xw, l_offs, S, U32)
+        xq_s = gather_codes("xq_s", xs, l_offs, S, U8)
+        w_w = deal_words("w_w", ww)
+        w_s = deal_bytes("w_s", ws, (slice(0, 1), slice(1, PACK)))
+        for t in range(PACK):
+            acc = bank("y_acc%d" % t, "bank%d" % t, [P, S])
+            product(acc[:], w_w, w_s, t, xq_w[:], xq_s[:])
+            if t < 2:
+                nc.scalar.activation(ys[t][:, :S], acc[:], COPY, scale=gain[:, t : t + 1])
+            else:
+                nc.vector.tensor_scalar(ys[t][:, :S], acc[:], gain[:, t : t + 1], None, ALU.mult)
+
+        hc_got = gather_codes("hc_got", xs, l_hc, C, U8, "")
+        hc_dealt = deal_bytes("hc_dealt", hc_got)
+        hc_s = sb("hc_s", [P, C], U8)
+        nc.vector.tensor_copy(hc_s[:].bitcast(I32), hc_dealt[:].bitcast(I32))
+        for r in range(2):
+            nc.sync.dma_start(hc_s[2 + r : P : 32, :].bitcast(I32), hc_dealt[16 + r : P : 32, :].bitcast(I32))
+
+        a_win = [sb("a%d" % t, [P, 2 * S], F32) for t in range(PACK)]
+        b_win = [sb("b%d" % t, [P, 2 * S], F32) for t in range(PACK)]
+        z = sb("z", [P, PACK, S], F32)
+        z_w = sb("z_w", [P, S], U32)
+        z_s = sb("z_s", [P, S], U8)
+        for t in range(2):
+            fetch(a_win[t][:, S:], ys[t], l1, everything)
+        for t in range(PACK):
+            first, second = a_win[t][:, S:], b_win[t][:, S:]
+            for i, cols in enumerate(pieces(Z_PIECES) if t == last_t else [everything]):
+                if t >= 2:
+                    fetch(first[:, cols], ys[t], l1, cols)
+                fetch(second[:, cols], ys[t], l2, cols)
+                nc.vector.scalar_tensor_tensor(z[:, t, cols], second[:, cols], 0.75, first[:, cols], ALU.mult, ALU.add)
+                if t == last_t:
+                    round_and_quantize("z_b%d" % i, z, cols, z_w, z_s)
+
+        ca_s = deal_bytes("ca_s", gather_codes("ca_s_got", xs, l_ca, C, U8))
+        ca_w = deal_words("ca_w", gather_codes("ca_w_got", xw, l_ca, C, U32))
+
+        early, late = pieces(Z_PIECES)
+        a_early = bank("a_early", "bank4", [P, PACK, early.stop - early.start])
+        for t in range(PACK):
+            product(a_early[:, t, :], ca_w, ca_s, t, z_w[:, early], z_s[:, early])
+        for t in range(PACK):
+            nc.scalar.activation(a_win[t][:, early], a_early[:, t, :], COPY, scale=0.0625)
+        for t in range(PACK):
+            acc = bank("a_late%d" % t, "bank%d" % t, [P, late.stop - late.start])
+            product(acc[:], ca_w, ca_s, t, z_w[:, late], z_s[:, late])
+            if t < 2:
+                nc.scalar.activation(a_win[t][:, late], acc[:], COPY, scale=0.0625)
+            else:
+                nc.vector.tensor_scalar(a_win[t][:, late], acc[:], 0.0625, None, ALU.mult)
+
+        hc_w = deal_words("hc_w", gather_codes("hc_w_got", xw, l_hc, C, U32, "z"))
+        for t in range(PACK):
+            acc = bank("b_acc%d" % t, "bank%d" % (4 + t), [P, S])
+            product(acc[:], hc_w, hc_s, t, z_w[:], z_s[:])
+            nc.vector.tensor_scalar(b_win[t][:, :S], acc[:], 0.0625, None, ALU.mult)
+
+        o_w = sb("o_w", [P, S], U32)
+        o_s = sb("o_s", [P, S], U8)
+        res = sb("res", [P, PACK, S], F32)
+        out_rows = out_0.rearrange("(p t) j -> p t j", t=PACK)
+        out_words = out_1[0].rearrange("p c r -> p (c r)").bitcast(I32)
+        steps = [(t, everything) for t in range(last_t)] + [(last_t, cols) for cols in pieces(OUT_PIECES)]
+        from_a = {}
+
+        def fetch_a(s, tag=""):
+            t, cols = steps[s]
+            from_a[s] = sb("from_a%d" % s, [P, 2, cols.stop - cols.start], F32, tag)
+            for u, lst in enumerate((l3, l4)):
+                fetch(from_a[s][:, u, :], a_win[t], lst, cols)
+
+        for s in range(2):
+            fetch_a(s)
+        for s, (t, cols) in enumerate(steps):
+            n = cols.stop - cols.start
+            if s >= 2:
+                fetch_a(s)
+            from_b = sb("from_b%d" % s, [P, 2, n], F32)
+            sums = sb("sums%d" % s, [P, 2, n], F32)
+            for u, lst in enumerate((l5, l6)):
+                fetch(from_b[:, u, :], b_win[t], lst, cols)
+            nc.vector.tensor_tensor(sums[:], from_a[s][:], from_b[:], ALU.add)
+            nc.vector.tensor_tensor(res[:, t, cols], sums[:, 0, :], sums[:, 1, :], ALU.max)
+            if cols.stop == S:
+                nc.sync.dma_start(out_rows[:, t, :], res[:, t, :])
+            if t == last_t:
+                round_and_quantize("res_b%d" % s, res, cols, o_w, o_s)
+                nc.sync.dma_start(out_words[:, cols], o_w[:, cols].bitcast(I32))
+        out_scales = out_2[0].bitcast(I32)
+        for q in range(4):
+            queue = nc.scalar if q % 2 == 0 else nc.sync
+            queue.dma_start(out_scales[4 * q : 4 * q + 4, :], o_s[32 * q : 32 * q + 4, :].bitcast(I32))

@@ -19,13 +19,8 @@ P = 128
 PACK = 4
 PER_COL = 16
 CODE_GATHER = 256
-Z_PIECES = [128,128]
-OUT_PIECES = [128,64,64]
-
-
-def pieces(widths):
-    starts = [sum(widths[:i]) for i in range(len(widths))]
-    return [slice(a, a + w) for a, w in zip(starts, widths)]
+ALL = slice(0, S)
+HALVES = (slice(0, S // 2), slice(S // 2, S))
 
 
 def offsets(lst, cols):
@@ -43,13 +38,62 @@ def tile_picked_cdhpathbsum_none_po_kernel(
         def sb(name, shape, dtype, tag=""):
             return keep.tile(shape, dtype, name=name, tag=tag or name, align_bytes=64)
 
-        def bank(name, tag, shape):
-            return psum.tile(shape, F32, name=name, tag=tag)
+        def bank(name, number, shape):
+            return psum.tile(shape, F32, name=name, tag="bank%d" % number)
 
         def load_list(name, src):
             lst = sb(name, [P, src.shape[1]], U16)
             nc.sync.dma_start(lst[:], src)
             return lst
+
+        def gather_codes(name, table, lst, n, dtype, tag=""):
+            got = sb(name, [P, n], dtype, tag)
+            for start in range(0, n, CODE_GATHER):
+                cols = slice(start, start + CODE_GATHER)
+                nc.vector.tensor_copy(got[:, cols], table[:].indirect(offsets(lst, cols)))
+            return got
+
+        def deal_words(name, src):
+            dealt = sb(name, [P, C], U32)
+            nc.vector.tensor_copy(
+                dealt[:].bitcast(I32).rearrange("p (t m) -> p m t", t=PACK),
+                src[:].bitcast(I32).rearrange("p (m t) -> p m t", t=PACK),
+            )
+            return dealt
+
+        def deal_bytes(name, src, groups=(slice(0, PACK),), tag="", engine=nc.vector):
+            dealt = sb(name, [P, C], U8, tag)
+            for ts in groups:
+                engine.tensor_copy(
+                    dealt[:].rearrange("p (t m) -> p t m", t=PACK)[:, ts, :],
+                    src[:].rearrange("p (m t) -> p t m", t=PACK)[:, ts, :],
+                )
+            return dealt
+
+        def product(out, words, scales, t, mov_words, mov_scales):
+            rows = slice(t * P, (t + 1) * P)
+            nc.tensor.matmul_mx(
+                out=out,
+                lhsT=words[:, rows].bitcast(FP8X4),
+                lhsT_scale=scales[:, rows],
+                rhs=mov_words.bitcast(FP8X4),
+                rhs_scale=mov_scales,
+                start=True,
+                stop=True,
+            )
+
+        def quantize(rounded, cols, words, scales):
+            nc.vector.quantize_mx(
+                out=words[:, cols].bitcast(FP8X4),
+                scales=scales[:, cols],
+                in_=rounded[:, cols, :].rearrange("p n t -> p (n t)"),
+            )
+
+        def fetch(dst, window, lst, cols):
+            nc.scalar.activation(dst, window[:].indirect(offsets(lst, cols)), COPY)
+
+        def side_by_side(pair, cols):
+            return pair[:, :, cols].rearrange("p t j -> p j t")
 
         xs = sb("xs", [P, T], U8)
         ws = sb("ws", [P, H], U8)
@@ -79,153 +123,121 @@ def tile_picked_cdhpathbsum_none_po_kernel(
         l5 = load_list("l5", n5)
         l6 = load_list("l6", n6)
 
-        def gather_codes(name, table, lst, n, dtype, tag=""):
-            got = sb(name, [P, n], dtype, tag)
-            for cols in pieces([CODE_GATHER] * (n // CODE_GATHER)):
-                nc.vector.tensor_copy(got[:, cols], table[:].indirect(offsets(lst, cols)))
-            return got
+        ys = [sb("y%d" % t, [P, 2 * S if t < 3 else S], F32) for t in range(PACK)]
+        nc.vector.memset(ys[0][:, S:], 0.0)
+        for t in (1, 2):
+            nc.scalar.activation(ys[t][:, S:], ys[0][:, S:], COPY)
+        hc_rows = sb("hc_rows", [P, C], U8)
+        nc.vector.memset(hc_rows[:].bitcast(I32), 0)
 
-        def deal_words(name, src):
-            dealt = sb(name, [P, C], U32)
-            nc.vector.tensor_copy(
-                dealt[:].bitcast(I32).rearrange("p (t m) -> p m t", t=PACK),
-                src[:].bitcast(I32).rearrange("p (m t) -> p m t", t=PACK),
-            )
-            return dealt
-
-        def deal_bytes(name, src, groups=(slice(0, PACK),)):
-            dealt = sb(name, [P, C], U8)
-            for ts in groups:
-                nc.vector.tensor_copy(
-                    dealt[:].rearrange("p (t m) -> p t m", t=PACK)[:, ts, :],
-                    src[:].rearrange("p (m t) -> p t m", t=PACK)[:, ts, :],
-                )
-            return dealt
-
-        def product(out, words, scales, t, mov_words, mov_scales):
-            rows = slice(t * P, (t + 1) * P)
-            nc.tensor.matmul_mx(
-                out=out,
-                lhsT=words[:, rows].bitcast(FP8X4),
-                lhsT_scale=scales[:, rows],
-                rhs=mov_words.bitcast(FP8X4),
-                rhs_scale=mov_scales,
-                start=True,
-                stop=True,
-            )
-
-        def round_and_quantize(name, planes, cols, words, scales):
-            rounded = sb(name, [P, cols.stop - cols.start, PACK], BF16)
-            nc.vector.tensor_copy(
-                rounded[:].rearrange("p (c i) t -> p c t i", i=4),
-                planes[:, :, cols].rearrange("p t (c i) -> p c t i", i=4),
-            )
-            nc.vector.quantize_mx(
-                out=words[:, cols].bitcast(FP8X4),
-                scales=scales[:, cols],
-                in_=rounded[:].rearrange("p n t -> p (n t)"),
-            )
-
-        def fetch(dst, window, lst, cols):
-            table = window[:] if cols.stop - cols.start >= P else window[:, :S]
-            nc.scalar.activation(dst, table.indirect(offsets(lst, cols)), COPY)
-
-        everything = slice(0, S)
-        last_t = PACK - 1
-
-        ys = [sb("y%d" % t, [P, 2 * S], F32) for t in range(PACK)]
-        for y in ys:
-            nc.vector.memset(y[:, S:], 0.0)
         xq_w = gather_codes("xq_w", xw, l_offs, S, U32)
         xq_s = gather_codes("xq_s", xs, l_offs, S, U8)
         w_w = deal_words("w_w", ww)
-        w_s = deal_bytes("w_s", ws, (slice(0, 1), slice(1, PACK)))
+        w_s = deal_bytes("w_s", ws, (slice(0, 1), slice(1, PACK)), engine=nc.vector)
         for t in range(PACK):
-            acc = bank("y_acc%d" % t, "bank%d" % t, [P, S])
+            acc = bank("y_acc%d" % t, t, [P, S])
             product(acc[:], w_w, w_s, t, xq_w[:], xq_s[:])
             if t < 2:
                 nc.scalar.activation(ys[t][:, :S], acc[:], COPY, scale=gain[:, t : t + 1])
             else:
                 nc.vector.tensor_scalar(ys[t][:, :S], acc[:], gain[:, t : t + 1], None, ALU.mult)
 
-        hc_got = gather_codes("hc_got", xs, l_hc, C, U8, "")
-        hc_dealt = deal_bytes("hc_dealt", hc_got)
-        hc_s = sb("hc_s", [P, C], U8)
-        nc.vector.tensor_copy(hc_s[:].bitcast(I32), hc_dealt[:].bitcast(I32))
-        for r in range(2):
-            nc.sync.dma_start(hc_s[2 + r : P : 32, :].bitcast(I32), hc_dealt[16 + r : P : 32, :].bitcast(I32))
+        hc_got = gather_codes("hc_got", xs, l_hc, C, U8)
+        for r, src in enumerate((0, 1, 16, 17)):
+            nc.sync.dma_start(hc_rows[r:P:32, :].bitcast(I32), hc_got[src:P:32, :].bitcast(I32))
 
-        a_win = [sb("a%d" % t, [P, 2 * S], F32) for t in range(PACK)]
-        b_win = [sb("b%d" % t, [P, 2 * S], F32) for t in range(PACK)]
-        z = sb("z", [P, PACK, S], F32)
+        wide = [sb("wide%d" % i, [P, 3 * S], F32) for i in range(4)]
+        a_win = [wide[0], wide[1], ys[0], sb("a3", [P, S], F32)]
+        b_win = [wide[2], wide[3], ys[1], sb("b3", [P, S], F32)]
+        first = [w[:, S:].rearrange("p (t j) -> p t j", t=2) for w in wide[:2]]
+        second = [w[:, S:].rearrange("p (t j) -> p t j", t=2) for w in wide[2:]]
+        z_b = sb("z_b", [P, S, PACK], BF16)
         z_w = sb("z_w", [P, S], U32)
         z_s = sb("z_s", [P, S], U8)
-        for t in range(2):
-            fetch(a_win[t][:, S:], ys[t], l1, everything)
-        for t in range(PACK):
-            first, second = a_win[t][:, S:], b_win[t][:, S:]
-            for i, cols in enumerate(pieces(Z_PIECES) if t == last_t else [everything]):
-                if t >= 2:
-                    fetch(first[:, cols], ys[t], l1, cols)
-                fetch(second[:, cols], ys[t], l2, cols)
-                nc.vector.scalar_tensor_tensor(z[:, t, cols], second[:, cols], 0.75, first[:, cols], ALU.mult, ALU.add)
-                if t == last_t:
-                    round_and_quantize("z_b%d" % i, z, cols, z_w, z_s)
+
+        def combine(pair, cols):
+            nc.vector.scalar_tensor_tensor(
+                z_b[:, cols, 2 * pair : 2 * pair + 2],
+                side_by_side(second[pair], cols),
+                0.75,
+                side_by_side(first[pair], cols),
+                ALU.mult,
+                ALU.add,
+            )
+
+        for dst, lst in ((first[0], l1), (second[0], l2)):
+            for t in range(2):
+                fetch(dst[:, t, :], ys[t], lst, ALL)
+        combine(0, ALL)
+        for dst, lst in ((first[1], l1), (second[1], l2)):
+            fetch(dst[:, 0, :], ys[2], lst, ALL)
+        for cols in HALVES:
+            for dst, lst in ((first[1], l1), (second[1], l2)):
+                fetch(dst[:, 1, cols], ys[3], lst, cols)
+            combine(1, cols)
+            quantize(z_b, cols, z_w, z_s)
 
         ca_s = deal_bytes("ca_s", gather_codes("ca_s_got", xs, l_ca, C, U8))
         ca_w = deal_words("ca_w", gather_codes("ca_w_got", xw, l_ca, C, U32))
 
-        early, late = pieces(Z_PIECES)
-        a_early = bank("a_early", "bank4", [P, PACK, early.stop - early.start])
+        early, late = HALVES
         for t in range(PACK):
-            product(a_early[:, t, :], ca_w, ca_s, t, z_w[:, early], z_s[:, early])
+            acc = bank("a_early%d" % t, 4 + t, [P, S // 2])
+            product(acc[:], ca_w, ca_s, t, z_w[:, early], z_s[:, early])
+            nc.scalar.activation(a_win[t][:, early], acc[:], COPY, scale=0.0625)
         for t in range(PACK):
-            nc.scalar.activation(a_win[t][:, early], a_early[:, t, :], COPY, scale=0.0625)
-        for t in range(PACK):
-            acc = bank("a_late%d" % t, "bank%d" % t, [P, late.stop - late.start])
+            acc = bank("a_late%d" % t, t, [P, S // 2])
             product(acc[:], ca_w, ca_s, t, z_w[:, late], z_s[:, late])
             if t < 2:
                 nc.scalar.activation(a_win[t][:, late], acc[:], COPY, scale=0.0625)
             else:
                 nc.vector.tensor_scalar(a_win[t][:, late], acc[:], 0.0625, None, ALU.mult)
 
-        hc_w = deal_words("hc_w", gather_codes("hc_w_got", xw, l_hc, C, U32, "z"))
+        hc_w = deal_words("hc_w", gather_codes("hc_w_got", xw, l_hc, C, U32, "z_b"))
+        hc_s = deal_bytes("hc_s", hc_rows, tag="y3")
         for t in range(PACK):
-            acc = bank("b_acc%d" % t, "bank%d" % (4 + t), [P, S])
+            acc = bank("b_acc%d" % t, 4 + t, [P, S])
             product(acc[:], hc_w, hc_s, t, z_w[:], z_s[:])
             nc.vector.tensor_scalar(b_win[t][:, :S], acc[:], 0.0625, None, ALU.mult)
 
         o_w = sb("o_w", [P, S], U32)
         o_s = sb("o_s", [P, S], U8)
         res = sb("res", [P, PACK, S], F32)
+        res_b = sb("res_b", [P, S, PACK], BF16)
+        from_a = sb("from_a", [P, PACK, 2, S], F32)
+        from_b = sb("from_b", [P, PACK, 2, S], F32)
+        sums = sb("sums", [P, PACK, 2, S], F32)
         out_rows = out_0.rearrange("(p t) j -> p t j", t=PACK)
         out_words = out_1[0].rearrange("p c r -> p (c r)").bitcast(I32)
-        steps = [(t, everything) for t in range(last_t)] + [(last_t, cols) for cols in pieces(OUT_PIECES)]
-        from_a = {}
 
-        def fetch_a(s, tag=""):
-            t, cols = steps[s]
-            from_a[s] = sb("from_a%d" % s, [P, 2, cols.stop - cols.start], F32, tag)
-            for u, lst in enumerate((l3, l4)):
-                fetch(from_a[s][:, u, :], a_win[t], lst, cols)
+        def fetch_both(dst, window, lists, t):
+            for u, lst in enumerate(lists):
+                fetch(dst[:, t, u, :], window[t], lst, ALL)
 
-        for s in range(2):
-            fetch_a(s)
-        for s, (t, cols) in enumerate(steps):
-            n = cols.stop - cols.start
-            if s >= 2:
-                fetch_a(s)
-            from_b = sb("from_b%d" % s, [P, 2, n], F32)
-            sums = sb("sums%d" % s, [P, 2, n], F32)
-            for u, lst in enumerate((l5, l6)):
-                fetch(from_b[:, u, :], b_win[t], lst, cols)
-            nc.vector.tensor_tensor(sums[:], from_a[s][:], from_b[:], ALU.add)
-            nc.vector.tensor_tensor(res[:, t, cols], sums[:, 0, :], sums[:, 1, :], ALU.max)
-            if cols.stop == S:
-                nc.sync.dma_start(out_rows[:, t, :], res[:, t, :])
-            if t == last_t:
-                round_and_quantize("res_b%d" % s, res, cols, o_w, o_s)
-                nc.sync.dma_start(out_words[:, cols], o_w[:, cols].bitcast(I32))
+        def larger(t, cols):
+            nc.vector.tensor_tensor(res[:, t, cols], sums[:, t, 0, cols], sums[:, t, 1, cols], ALU.max)
+
+        for t in range(3):
+            fetch_both(from_a, a_win, (l3, l4), t)
+        for t in range(3):
+            fetch_both(from_b, b_win, (l5, l6), t)
+            nc.vector.tensor_tensor(sums[:, t], from_a[:, t], from_b[:, t], ALU.add)
+            larger(t, ALL)
+            nc.sync.dma_start(out_rows[:, t, :], res[:, t, :])
+            if t == 1:
+                nc.vector.tensor_copy(res_b[:, :, 0:2], side_by_side(res[:, 0:2, :], ALL))
+        for cols in HALVES:
+            for u, (list_a, list_b) in enumerate(((l3, l5), (l4, l6))):
+                fetch(from_a[:, 3, u, cols], a_win[3], list_a, cols)
+                fetch(from_b[:, 3, u, cols], b_win[3], list_b, cols)
+                nc.vector.tensor_tensor(sums[:, 3, u, cols], from_a[:, 3, u, cols], from_b[:, 3, u, cols], ALU.add)
+            nc.vector.tensor_tensor(
+                res_b[:, cols, 2:4], side_by_side(sums[:, 2:4, 0, :], cols), side_by_side(sums[:, 2:4, 1, :], cols), ALU.max
+            )
+            larger(3, cols)
+            quantize(res_b, cols, o_w, o_s)
+            nc.sync.dma_start(out_rows[:, 3, cols], res[:, 3, cols])
+            nc.sync.dma_start(out_words[:, cols], o_w[:, cols].bitcast(I32))
         out_scales = out_2[0].bitcast(I32)
         for q in range(4):
             queue = nc.scalar if q % 2 == 0 else nc.sync

@@ -133,11 +133,11 @@ def tile_picked_cdhpathbsum_none_po_kernel(
         xq_w = gather_codes("xq_w", xw, l_offs, S, U32)
         xq_s = gather_codes("xq_s", xs, l_offs, S, U8)
         w_w = deal_words("w_w", ww)
-        w_s = deal_bytes("w_s", ws, (slice(0, 1), slice(1, PACK)), engine=nc.vector)
+        w_s = deal_bytes("w_s", ws, (slice(0, 1), slice(1, PACK)), engine=nc.gpsimd)
         for t in range(PACK):
             acc = bank("y_acc%d" % t, t, [P, S])
             product(acc[:], w_w, w_s, t, xq_w[:], xq_s[:])
-            if t < 2:
+            if t == 0:
                 nc.scalar.activation(ys[t][:, :S], acc[:], COPY, scale=gain[:, t : t + 1])
             else:
                 nc.vector.tensor_scalar(ys[t][:, :S], acc[:], gain[:, t : t + 1], None, ALU.mult)
@@ -180,18 +180,18 @@ def tile_picked_cdhpathbsum_none_po_kernel(
         ca_s = deal_bytes("ca_s", gather_codes("ca_s_got", xs, l_ca, C, U8))
         ca_w = deal_words("ca_w", gather_codes("ca_w_got", xw, l_ca, C, U32))
 
-        early, late = HALVES
-        for t in range(PACK):
-            acc = bank("a_early%d" % t, 4 + t, [P, S // 2])
-            product(acc[:], ca_w, ca_s, t, z_w[:, early], z_s[:, early])
-            nc.scalar.activation(a_win[t][:, early], acc[:], COPY, scale=0.0625)
-        for t in range(PACK):
-            acc = bank("a_late%d" % t, t, [P, S // 2])
-            product(acc[:], ca_w, ca_s, t, z_w[:, late], z_s[:, late])
-            if t < 2:
-                nc.scalar.activation(a_win[t][:, late], acc[:], COPY, scale=0.0625)
-            else:
-                nc.vector.tensor_scalar(a_win[t][:, late], acc[:], 0.0625, None, ALU.mult)
+        for h, cols in enumerate(HALVES):
+            for t in range(2):
+                acc = bank("a_half%d_%d" % (h, t), 4 + 2 * h + t, [P, S // 2])
+                product(acc[:], ca_w, ca_s, t, z_w[:, cols], z_s[:, cols])
+                if (h, t) == (1, 1):
+                    nc.vector.tensor_scalar(a_win[t][:, cols], acc[:], 0.0625, None, ALU.mult)
+                else:
+                    nc.scalar.activation(a_win[t][:, cols], acc[:], COPY, scale=0.0625)
+        for t in range(2, PACK):
+            acc = bank("a_acc%d" % t, t, [P, S])
+            product(acc[:], ca_w, ca_s, t, z_w[:], z_s[:])
+            nc.vector.tensor_scalar(a_win[t][:, :S], acc[:], 0.0625, None, ALU.mult)
 
         hc_w = deal_words("hc_w", gather_codes("hc_w_got", xw, l_hc, C, U32, "z_b"))
         hc_s = deal_bytes("hc_s", hc_rows, tag="y3")
@@ -204,33 +204,35 @@ def tile_picked_cdhpathbsum_none_po_kernel(
         o_s = sb("o_s", [P, S], U8)
         res = sb("res", [P, PACK, S], F32)
         res_b = sb("res_b", [P, S, PACK], BF16)
-        from_a = sb("from_a", [P, PACK, 2, S], F32)
+        from_a = sb("from_a", [P, 2, 2, S], F32)
         from_b = sb("from_b", [P, PACK, 2, S], F32)
         sums = sb("sums", [P, PACK, 2, S], F32)
         out_rows = out_0.rearrange("(p t) j -> p t j", t=PACK)
         out_words = out_1[0].rearrange("p c r -> p (c r)").bitcast(I32)
 
-        def fetch_both(dst, window, lists, t):
+        def fetch_both(dst, window, lists):
             for u, lst in enumerate(lists):
-                fetch(dst[:, t, u, :], window[t], lst, ALL)
+                fetch(dst[:, u, :], window, lst, ALL)
 
         def larger(t, cols):
             nc.vector.tensor_tensor(res[:, t, cols], sums[:, t, 0, cols], sums[:, t, 1, cols], ALU.max)
 
+        for t in range(2):
+            fetch_both(from_a[:, t], a_win[t], (l3, l4))
         for t in range(3):
-            fetch_both(from_a, a_win, (l3, l4), t)
-        for t in range(3):
-            fetch_both(from_b, b_win, (l5, l6), t)
-            nc.vector.tensor_tensor(sums[:, t], from_a[:, t], from_b[:, t], ALU.add)
+            if t == 2:
+                fetch_both(from_a[:, 0], a_win[t], (l3, l4))
+            fetch_both(from_b[:, t], b_win[t], (l5, l6))
+            nc.vector.tensor_tensor(sums[:, t], from_a[:, t % 2], from_b[:, t], ALU.add)
             larger(t, ALL)
             nc.sync.dma_start(out_rows[:, t, :], res[:, t, :])
             if t == 1:
                 nc.vector.tensor_copy(res_b[:, :, 0:2], side_by_side(res[:, 0:2, :], ALL))
         for cols in HALVES:
             for u, (list_a, list_b) in enumerate(((l3, l5), (l4, l6))):
-                fetch(from_a[:, 3, u, cols], a_win[3], list_a, cols)
+                fetch(from_a[:, 1, u, cols], a_win[3], list_a, cols)
                 fetch(from_b[:, 3, u, cols], b_win[3], list_b, cols)
-                nc.vector.tensor_tensor(sums[:, 3, u, cols], from_a[:, 3, u, cols], from_b[:, 3, u, cols], ALU.add)
+                nc.vector.tensor_tensor(sums[:, 3, u, cols], from_a[:, 1, u, cols], from_b[:, 3, u, cols], ALU.add)
             nc.vector.tensor_tensor(
                 res_b[:, cols, 2:4], side_by_side(sums[:, 2:4, 0, :], cols), side_by_side(sums[:, 2:4, 1, :], cols), ALU.max
             )

@@ -133,7 +133,7 @@ def tile_picked_cdhpathbsum_none_po_kernel(
         xq_w = gather_codes("xq_w", xw, l_offs, S, U32)
         xq_s = gather_codes("xq_s", xs, l_offs, S, U8)
         w_w = deal_words("w_w", ww)
-        w_s = deal_bytes("w_s", ws, (slice(0, 1), slice(1, PACK)), engine=nc.gpsimd)
+        w_s = deal_bytes("w_s", ws, (slice(0, 1), slice(1, PACK)), engine=nc.vector)
         for t in range(PACK):
             acc = bank("y_acc%d" % t, t, [P, S])
             product(acc[:], w_w, w_s, t, xq_w[:], xq_s[:])
@@ -204,7 +204,7 @@ def tile_picked_cdhpathbsum_none_po_kernel(
         o_s = sb("o_s", [P, S], U8)
         res = sb("res", [P, PACK, S], F32)
         res_b = sb("res_b", [P, S, PACK], BF16)
-        from_a = sb("from_a", [P, 2, 2, S], F32)
+        from_a = sb("from_a", [P, 3, 2, S], F32)
         from_b = sb("from_b", [P, PACK, 2, S], F32)
         sums = sb("sums", [P, PACK, 2, S], F32)
         out_rows = out_0.rearrange("(p t) j -> p t j", t=PACK)
@@ -217,13 +217,11 @@ def tile_picked_cdhpathbsum_none_po_kernel(
         def larger(t, cols):
             nc.vector.tensor_tensor(res[:, t, cols], sums[:, t, 0, cols], sums[:, t, 1, cols], ALU.max)
 
-        for t in range(2):
+        for t in range(3):
             fetch_both(from_a[:, t], a_win[t], (l3, l4))
         for t in range(3):
-            if t == 2:
-                fetch_both(from_a[:, 0], a_win[t], (l3, l4))
             fetch_both(from_b[:, t], b_win[t], (l5, l6))
-            nc.vector.tensor_tensor(sums[:, t], from_a[:, t % 2], from_b[:, t], ALU.add)
+            nc.vector.tensor_tensor(sums[:, t], from_a[:, t], from_b[:, t], ALU.add)
             larger(t, ALL)
             nc.sync.dma_start(out_rows[:, t, :], res[:, t, :])
             if t == 1:

from contextlib import ExitStack

import concourse.mybir as mybir

K, T, S, H, C = 512, 2048, 256, 512, 512
FLOPS = 2 * K * S * (H + 2 * C)

F32 = mybir.dt.float32
BF16 = mybir.dt.bfloat16
I32 = mybir.dt.int32
U32 = mybir.dt.uint32
U16 = mybir.dt.uint16
U8 = mybir.dt.uint8
FP8X4 = mybir.dt.float8_e4m3fn_x4
COPY = mybir.ActivationFunctionType.Copy
ALU = mybir.AluOpType

P = 128
PACK = 4
PER_COL = 16
CODE_GATHER = 256
ALL = slice(0, S)
HALVES = (slice(0, S // 2), slice(S // 2, S))


def offsets(lst, cols):
    return lst[:, cols.start // PER_COL : cols.stop // PER_COL]


def tile_picked_cdhpathbsum_none_po_kernel(
    tc, x_words, x_scales, w1_words, w1_scales, gs, offs, n1, n2, ca, hc, n3, n4, n5, n6, out_0, out_1, out_2
):
    nc = tc.nc
    with ExitStack() as ctx:
        keep = ctx.enter_context(tc.tile_pool(name="keep", bufs=1))
        psum = ctx.enter_context(tc.psum_pool(name="psum", bufs=1))

        def sb(name, shape, dtype, tag=""):
            return keep.tile(shape, dtype, name=name, tag=tag or name, align_bytes=64)

        def bank(name, number, shape):
            return psum.tile(shape, F32, name=name, tag="bank%d" % number)

        def load_list(name, src):
            lst = sb(name, [P, src.shape[1]], U16)
            nc.sync.dma_start(lst[:], src)
            return lst

        def gather_codes(name, table, lst, n, dtype, tag=""):
            got = sb(name, [P, n], dtype, tag)
            for start in range(0, n, CODE_GATHER):
                cols = slice(start, start + CODE_GATHER)
                nc.vector.tensor_copy(got[:, cols], table[:].indirect(offsets(lst, cols)))
            return got

        def deal_words(name, src):
            dealt = sb(name, [P, C], U32)
            nc.vector.tensor_copy(
                dealt[:].bitcast(I32).rearrange("p (t m) -> p m t", t=PACK),
                src[:].bitcast(I32).rearrange("p (m t) -> p m t", t=PACK),
            )
            return dealt

        def deal_bytes(name, src, groups=(slice(0, PACK),), tag="", engine=nc.vector):
            dealt = sb(name, [P, C], U8, tag)
            for ts in groups:
                engine.tensor_copy(
                    dealt[:].rearrange("p (t m) -> p t m", t=PACK)[:, ts, :],
                    src[:].rearrange("p (m t) -> p t m", t=PACK)[:, ts, :],
                )
            return dealt

        def product(out, words, scales, t, mov_words, mov_scales):
            rows = slice(t * P, (t + 1) * P)
            nc.tensor.matmul_mx(
                out=out,
                lhsT=words[:, rows].bitcast(FP8X4),
                lhsT_scale=scales[:, rows],
                rhs=mov_words.bitcast(FP8X4),
                rhs_scale=mov_scales,
                start=True,
                stop=True,
            )

        def quantize(rounded, cols, words, scales):
            nc.vector.quantize_mx(
                out=words[:, cols].bitcast(FP8X4),
                scales=scales[:, cols],
                in_=rounded[:, cols, :].rearrange("p n t -> p (n t)"),
            )

        def fetch(dst, window, lst, cols):
            nc.scalar.activation(dst, window[:].indirect(offsets(lst, cols)), COPY)

        def side_by_side(pair, cols):
            return pair[:, :, cols].rearrange("p t j -> p j t")

        xs = sb("xs", [P, T], U8)
        ws = sb("ws", [P, H], U8)
        xw = sb("xw", [P, T], U32)
        ww = sb("ww", [P, H], U32)
        gain = sb("gain", [P, PACK], F32)
        nc.vector.memset(xs[:].bitcast(I32), 0)
        nc.vector.memset(ws[:].bitcast(I32), 0)
        xs_rows = x_scales[0].bitcast(I32)
        ws_rows = w1_scales[0].bitcast(I32)
        l_offs = load_list("l_offs", offs)
        l_hc = load_list("l_hc", hc)
        nc.sync.dma_start(ww[:].bitcast(I32), w1_words[0].rearrange("p c r -> p (c r)").bitcast(I32))
        nc.scalar.dma_start(xs[0:P:16, :].bitcast(I32), xs_rows[0:16:2, :])
        nc.sync.dma_start(xs[1:P:16, :].bitcast(I32), xs_rows[1:16:2, :])
        nc.scalar.dma_start(xs[2:P:32, :].bitcast(I32), xs_rows[2:16:4, :])
        nc.sync.dma_start(xs[3:P:32, :].bitcast(I32), xs_rows[3:16:4, :])
        nc.sync.dma_start(xw[:].bitcast(I32), x_words[0].rearrange("p c r -> p (c r)").bitcast(I32))
        for q in range(4):
            nc.sync.dma_start(ws[32 * q : 32 * q + 4, :].bitcast(I32), ws_rows[4 * q : 4 * q + 4, :])
        nc.sync.dma_start(gain[:], gs.rearrange("(p t) o -> p (t o)", t=PACK))
        l1 = load_list("l1", n1)
        l_ca = load_list("l_ca", ca)
        l2 = load_list("l2", n2)
        l3 = load_list("l3", n3)
        l4 = load_list("l4", n4)
        l5 = load_list("l5", n5)
        l6 = load_list("l6", n6)

        ys = [sb("y%d" % t, [P, 2 * S if t < 3 else S], F32) for t in range(PACK)]
        nc.vector.memset(ys[0][:, S:], 0.0)
        for t in (1, 2):
            nc.scalar.activation(ys[t][:, S:], ys[0][:, S:], COPY)
        hc_rows = sb("hc_rows", [P, C], U8)
        nc.vector.memset(hc_rows[:].bitcast(I32), 0)

        xq_w = gather_codes("xq_w", xw, l_offs, S, U32)
        xq_s = gather_codes("xq_s", xs, l_offs, S, U8)
        w_w = deal_words("w_w", ww)
        w_s = deal_bytes("w_s", ws, (slice(0, 1), slice(1, PACK)), engine=nc.vector)
        for t in range(PACK):
            acc = bank("y_acc%d" % t, t, [P, S])
            product(acc[:], w_w, w_s, t, xq_w[:], xq_s[:])
            if t == 0:
                nc.scalar.activation(ys[t][:, :S], acc[:], COPY, scale=gain[:, t : t + 1])
            else:
                nc.vector.tensor_scalar(ys[t][:, :S], acc[:], gain[:, t : t + 1], None, ALU.mult)

        hc_got = gather_codes("hc_got", xs, l_hc, C, U8)
        for r, src in enumerate((0, 1, 16, 17)):
            nc.sync.dma_start(hc_rows[r:P:32, :].bitcast(I32), hc_got[src:P:32, :].bitcast(I32))

        wide = [sb("wide%d" % i, [P, 3 * S], F32) for i in range(4)]
        a_win = [wide[0], wide[1], ys[0], sb("a3", [P, S], F32)]
        b_win = [wide[2], wide[3], ys[1], sb("b3", [P, S], F32)]
        first = [w[:, S:].rearrange("p (t j) -> p t j", t=2) for w in wide[:2]]
        second = [w[:, S:].rearrange("p (t j) -> p t j", t=2) for w in wide[2:]]
        z_b = sb("z_b", [P, S, PACK], BF16)
        z_w = sb("z_w", [P, S], U32)
        z_s = sb("z_s", [P, S], U8)

        def combine(pair, cols):
            nc.vector.scalar_tensor_tensor(
                z_b[:, cols, 2 * pair : 2 * pair + 2],
                side_by_side(second[pair], cols),
                0.75,
                side_by_side(first[pair], cols),
                ALU.mult,
                ALU.add,
            )

        for dst, lst in ((first[0], l1), (second[0], l2)):
            for t in range(2):
                fetch(dst[:, t, :], ys[t], lst, ALL)
        combine(0, ALL)
        for dst, lst in ((first[1], l1), (second[1], l2)):
            fetch(dst[:, 0, :], ys[2], lst, ALL)
        for cols in HALVES:
            for dst, lst in ((first[1], l1), (second[1], l2)):
                fetch(dst[:, 1, cols], ys[3], lst, cols)
            combine(1, cols)
            quantize(z_b, cols, z_w, z_s)

        ca_s = deal_bytes("ca_s", gather_codes("ca_s_got", xs, l_ca, C, U8))
        ca_w = deal_words("ca_w", gather_codes("ca_w_got", xw, l_ca, C, U32))

        for h, cols in enumerate(HALVES):
            for t in range(2):
                acc = bank("a_half%d_%d" % (h, t), 4 + 2 * h + t, [P, S // 2])
                product(acc[:], ca_w, ca_s, t, z_w[:, cols], z_s[:, cols])
                if (h, t) == (1, 1):
                    nc.vector.tensor_scalar(a_win[t][:, cols], acc[:], 0.0625, None, ALU.mult)
                else:
                    nc.scalar.activation(a_win[t][:, cols], acc[:], COPY, scale=0.0625)
        for t in range(2, PACK):
            acc = bank("a_acc%d" % t, t, [P, S])
            product(acc[:], ca_w, ca_s, t, z_w[:], z_s[:])
            nc.vector.tensor_scalar(a_win[t][:, :S], acc[:], 0.0625, None, ALU.mult)

        hc_w = deal_words("hc_w", gather_codes("hc_w_got", xw, l_hc, C, U32, "z_b"))
        hc_s = deal_bytes("hc_s", hc_rows, tag="y3")
        for t in range(PACK):
            acc = bank("b_acc%d" % t, 4 + t, [P, S])
            product(acc[:], hc_w, hc_s, t, z_w[:], z_s[:])
            nc.vector.tensor_scalar(b_win[t][:, :S], acc[:], 0.0625, None, ALU.mult)

        o_w = sb("o_w", [P, S], U32)
        o_s = sb("o_s", [P, S], U8)
        res = sb("res", [P, PACK, S], F32)
        res_b = sb("res_b", [P, S, PACK], BF16)
        from_a = sb("from_a", [P, 3, 2, S], F32)
        from_b = sb("from_b", [P, PACK, 2, S], F32)
        sums = sb("sums", [P, PACK, 2, S], F32)
        out_rows = out_0.rearrange("(p t) j -> p t j", t=PACK)
        out_words = out_1[0].rearrange("p c r -> p (c r)").bitcast(I32)

        def fetch_both(dst, window, lists):
            for u, lst in enumerate(lists):
                fetch(dst[:, u, :], window, lst, ALL)

        def larger(t, cols):
            nc.vector.tensor_tensor(res[:, t, cols], sums[:, t, 0, cols], sums[:, t, 1, cols], ALU.max)

        for t in range(3):
            fetch_both(from_a[:, t], a_win[t], (l3, l4))
        for t in range(3):
            fetch_both(from_b[:, t], b_win[t], (l5, l6))
            nc.vector.tensor_tensor(sums[:, t], from_a[:, t], from_b[:, t], ALU.add)
            larger(t, ALL)
            nc.sync.dma_start(out_rows[:, t, :], res[:, t, :])
            if t == 1:
                nc.vector.tensor_copy(res_b[:, :, 0:2], side_by_side(res[:, 0:2, :], ALL))
        for cols in HALVES:
            for u, (list_a, list_b) in enumerate(((l3, l5), (l4, l6))):
                fetch(from_a[:, 1, u, cols], a_win[3], list_a, cols)
                fetch(from_b[:, 3, u, cols], b_win[3], list_b, cols)
                nc.vector.tensor_tensor(sums[:, 3, u, cols], from_a[:, 1, u, cols], from_b[:, 3, u, cols], ALU.add)
            nc.vector.tensor_tensor(
                res_b[:, cols, 2:4], side_by_side(sums[:, 2:4, 0, :], cols), side_by_side(sums[:, 2:4, 1, :], cols), ALU.max
            )
            larger(3, cols)
            quantize(res_b, cols, o_w, o_s)
            nc.sync.dma_start(out_rows[:, 3, cols], res[:, 3, cols])
            nc.sync.dma_start(out_words[:, cols], o_w[:, cols].bitcast(I32))
        out_scales = out_2[0].bitcast(I32)
        for q in range(4):
            queue = nc.scalar if q % 2 == 0 else nc.sync
            queue.dma_start(out_scales[4 * q : 4 * q + 4, :], o_s[32 * q : 32 * q + 4, :].bitcast(I32))
